import numpy as np
import ml_dtypes


def mxq(x, axis, fmt="e4m3"):
    dtype, down = {"e4m3": (ml_dtypes.float8_e4m3fn, 7), "e5m2": (ml_dtypes.float8_e5m2, 14)}[fmt]
    v = np.moveaxis(np.asarray(x, np.float32).astype(ml_dtypes.bfloat16).astype(np.float64), axis, -1)
    blocks = v.reshape(v.shape[:-1] + (-1, 32))
    amax = np.abs(blocks).max(-1, keepdims=True)
    byte = np.maximum(np.where(amax > 0, np.frexp(amax)[1] - 1 + 127, 0) - down, 1)
    scale = np.exp2(byte - 127.0)
    codes = (blocks / scale).astype(np.float32).astype(dtype).astype(np.float64)
    return np.moveaxis((codes * scale).reshape(v.shape), -1, axis)


WIDE = False


def mx_kscale(k):
    if not WIDE:
        return np.ones(k)
    levels = np.array([10, -10, 5, -5, 0])
    if k % 512:
        return np.exp2(np.random.permutation(np.resize(levels, k // 32))).repeat(32)
    a = np.empty((k // 512, 16))
    for p in range(k // 512):
        a[p, :8] = np.random.permutation(np.resize(levels, 8))
        for g in range(8):
            far = levels[np.abs(levels - a[p, g]) >= 10]
            a[p, g + 8] = far[np.random.randint(len(far))]
    return np.exp2(a.ravel()).repeat(32)


def f64(x):
    return np.asarray(x).astype(np.float64)


def striped(idx):
    return np.tile(np.asarray(idx).reshape(-1, 16).T, (8, 1)).astype(np.uint16)


def unstriped(offs):
    return offs[:16].T.reshape(-1).astype(np.int64)


B, N, T, D, DV, NQ = 4, 256, 2048, 512, 0, 128
PAGE = 32
SEG = 32


def setup_inputs():
    n = np.random.standard_normal
    pages = np.random.permutation(T // PAGE)[:B * N // PAGE]
    idx = (pages[:, None] * PAGE + np.arange(PAGE)[None, :]).reshape(-1)
    s = mx_kscale(D)[:, None]
    r = np.random.uniform(0.5, 2.0, T)
    return {
        "qT": (n((B, D, NQ)) * s * (1.00 / np.sqrt(D))).astype(np.float32),
        "kT": (n((D, T)) / s / r).astype(np.float32),
        "ts": np.tile(r, (128, 1)).astype(np.float32),
        "kb": np.tile(n(T), (128, 1)).astype(np.float32),
        "offs": striped(idx),
    }


def reference(qT, kT, ts, kb, offs):
    idx = unstriped(offs)
    pick = lambda x: x[:, idx].reshape(x.shape[0], B, N).transpose(1, 0, 2)
    a = mxq(f64(qT), 1, "e4m3").transpose(0, 2, 1) @ mxq(pick(f64(kT)), 1, "e4m3")
    a = a * pick(f64(ts))[:, :1, :]
    a = a + pick(f64(kb))[:, :1, :]
    return a.reshape(B, NQ, N // SEG, SEG).max(-1)

from contextlib import ExitStack

import concourse.mybir as mybir
from concourse.masks import make_identity

F32 = mybir.dt.float32
BF16 = mybir.dt.bfloat16
U32 = mybir.dt.uint32
U16 = mybir.dt.uint16
U8 = mybir.dt.uint8
FP8X4 = mybir.dt.float8_e4m3fn_x4
COPY = mybir.ActivationFunctionType.Copy
IDENT = mybir.ActivationFunctionType.Identity
MAX = mybir.AluOpType.max
X = mybir.AxisListType.X

B, N, T, D, NQ = 4, 256, 2048, 512, 128
P = 128
FLOPS = 2 * B * NQ * N * D
HALVES = N // P


def tile_attend_maxsim_tskb_kernel(tc, qT, kT, ts, kb, offs, out):
    nc = tc.nc
    with ExitStack() as ctx:
        held = ctx.enter_context(tc.tile_pool(name="held", bufs=1))
        psum_mm = ctx.enter_context(tc.psum_pool(name="psum_mm", bufs=4))
        psum_t = ctx.enter_context(tc.psum_pool(name="psum_t", bufs=2))
        psum_c = ctx.enter_context(tc.psum_pool(name="psum_c", bufs=2))
        work = ctx.enter_context(tc.tile_pool(name="work", bufs=4))

        offsets = held.tile([P, B * N // 16], U16, name="offsets")
        nc.sync.dma_start(offsets[:], offs)

        ts_win = held.tile([P, T], F32, name="ts_win")
        kb_win = held.tile([P, T], F32, name="kb_win")
        nc.vector.memset(ts_win[:], 0.0)
        nc.gpsimd.memset(kb_win[:], 0.0)

        k_rows = kT.rearrange("(p t) w -> p t w", t=4)
        planes = []
        for t in range(4):
            plane = held.tile([P, T], F32, name="plane%d" % t)
            nc.sync.dma_start(plane[:], k_rows[:, t, :])
            if t == 0:
                nc.sync.dma_start(ts_win[0:1, :], ts[0:1, :])
                nc.sync.dma_start(kb_win[0:1, :], kb[0:1, :])
            planes.append(plane)

        q_raws = []
        for h in range(2):
            q_raw = held.tile([P, 2, 4 * NQ], F32, name="q_raw%d" % h)
            nc.sync.dma_start(q_raw[:], qT[2 * h : 2 * h + 2].rearrange("b (p t) q -> p b (t q)", t=4))
            q_raws.append(q_raw)

        ident = held.tile([P, P], F32, name="ident")
        make_identity(nc, ident[:])

        warm = held.tile([P, 8], F32, name="warm")
        nc.vector.memset(warm[:], 0.0)
        warm2 = held.tile([P, 8], F32, name="warm2")
        nc.scalar.activation(warm2[:], warm[:], IDENT)

        cols = []
        for name, win in (("ts", ts_win), ("kb", kb_win)):
            picked = held.tile([P, B * N], F32, name=name + "_picked")
            nc.vector.tensor_copy(picked[:], win[:].indirect(offsets[:]))
            col = held.tile([P, 8], F32, name=name + "_col")
            for half in range(2):
                bank = psum_c.tile([P, 4, P], F32, name="bank_c")
                for j in range(4):
                    k = 4 * half + j
                    nc.tensor.transpose(bank[:, j, :], picked[:, k * P : (k + 1) * P], ident[:])
                nc.scalar.copy(col[:, 4 * half : 4 * half + 4], bank[:, :, 0])
            cols.append(col)
        ts_col, kb_col = cols

        raw = held.tile([P, 4, B * N], F32, name="raw")
        grouped = [held.tile([P, N, 4], BF16, name="grouped%d" % b, align_bytes=64) for b in range(B)]
        for t in range(3):
            nc.vector.tensor_copy(raw[:, t, :], planes[t][:].indirect(offsets[:]))
        for b in range(B):
            nc.scalar.activation(grouped[b][:, :, 0:2], raw[:, 0:2, b * N : (b + 1) * N].rearrange("p t n -> p n t"), COPY)
        for b in range(B):
            nc.vector.tensor_copy(
                raw[:, 3, b * N : (b + 1) * N],
                planes[3][:].indirect(offsets[:, b * (N // 16) : (b + 1) * (N // 16)]),
            )
        k_codes, k_scales = [], []
        q_codes, q_scales = [], []
        for b in range(B):
            src = raw[:, 2:4, b * N : (b + 1) * N].rearrange("p t n -> p n t")
            if b % 2 == 0:
                nc.scalar.activation(grouped[b][:, :, 2:4], src, COPY)
            else:
                nc.vector.tensor_copy(grouped[b][:, :, 2:4], src)
            if b % 2 == 0:
                h = b // 2
                q_grouped = held.tile([P, 2, NQ, 4], BF16, name="q_grouped%d" % h, align_bytes=64)
                nc.scalar.activation(
                    q_grouped[:], q_raws[h][:].rearrange("p b (t q) -> p b q t", t=4), COPY
                )
                qc = held.tile([P, 2 * NQ], U32, name="q_codes%d" % h, align_bytes=64)
                qs = held.tile([P, 2 * NQ], U8, name="q_scales%d" % h, align_bytes=64)
                nc.vector.quantize_mx(
                    out=qc[:].bitcast(FP8X4), scales=qs[:], in_=q_grouped[:].rearrange("p b q t -> p (b q t)")
                )
                q_codes.append(qc)
                q_scales.append(qs)
            kc = held.tile([P, N], U32, name="k_codes%d" % b, align_bytes=64)
            ks = held.tile([P, N], U8, name="k_scales%d" % b, align_bytes=64)
            nc.vector.quantize_mx(
                out=kc[:].bitcast(FP8X4), scales=ks[:], in_=grouped[b][:].rearrange("p n t -> p (n t)")
            )
            k_codes.append(kc)
            k_scales.append(ks)

        for b in range(B):
            turned = psum_t.tile([P, N], F32, name="turned")
            q_cols = slice((b % 2) * NQ, (b % 2 + 1) * NQ)
            for half in range(HALVES):
                acc = psum_mm.tile([P, NQ], F32, name="acc")
                s_cols = slice(half * P, (half + 1) * P)
                nc.tensor.matmul_mx(
                    out=acc[:],
                    lhsT=k_codes[b][:, s_cols].bitcast(FP8X4),
                    lhsT_scale=k_scales[b][:, s_cols],
                    rhs=q_codes[b // 2][:, q_cols].bitcast(FP8X4),
                    rhs_scale=q_scales[b // 2][:, q_cols],
                    start=True,
                    stop=True,
                )
                k = HALVES * b + half
                scored = work.tile([P, NQ], F32, name="scored")
                nc.scalar.activation(scored[:], acc[:], IDENT, bias=kb_col[:, k : k + 1], scale=ts_col[:, k : k + 1])
                nc.tensor.transpose(turned[:, s_cols], scored[:], ident[:])
            best = work.tile([P, N // 32], F32, name="best")
            nc.vector.tensor_reduce(out=best[:], in_=turned[:].rearrange("p (j s) -> p j s", s=32), axis=X, op=MAX)
            nc.sync.dma_start(out[b], best[:])
